import numpy as np
CORES = [0,1,2,3]
N = 4
T = 32
ROUTE = [[[2,1],[2,1],[3,0],[3,0],[1,2],[1,0],[2,1],[1,0],[0,1],[1,0],[0,3],[0,1],[1,0],[1,0],[1,2],[0,2],[3,0],[1,0],[1,2],[2,0],[1,0],[3,2],[1,3],[3,0],[0,2],[1,0],[1,0],[2,0],[2,0],[1,0],[0,2],[2,1]],[[2,0],[2,3],[0,3],[3,0],[0,2],[3,0],[0,3],[2,1],[1,0],[3,1],[2,3],[2,0],[3,2],[3,2],[0,1],[1,0],[3,0],[1,2],[1,0],[1,2],[1,2],[1,3],[1,3],[1,0],[2,0],[3,1],[2,1],[3,2],[1,3],[0,3],[2,1],[3,0]],[[0,3],[3,2],[0,1],[2,1],[3,1],[3,0],[2,3],[3,0],[2,3],[2,1],[2,3],[0,2],[0,2],[1,3],[1,3],[3,0],[2,3],[3,2],[2,0],[3,2],[1,3],[3,0],[0,2],[3,2],[2,0],[0,2],[2,1],[2,1],[1,2],[3,0],[1,0],[1,2]],[[3,2],[0,2],[3,2],[0,2],[3,1],[2,0],[2,1],[2,3],[3,0],[0,1],[3,0],[3,1],[2,0],[3,2],[3,2],[0,2],[0,3],[3,0],[0,1],[2,3],[0,1],[2,0],[3,0],[1,3],[2,3],[0,1],[2,1],[1,2],[2,0],[2,0],[1,3],[2,3]]]
ZW = 70
def setup_inputs(rng):
    return {"z": rng.standard_normal((N, 128, ZW), dtype=np.float32)}
def reference(z):
    y = np.zeros((N, 128, T), np.float64)
    fill = [0] * N
    for r in range(N):
        for t in range(T):
            for e in ROUTE[r][t]:
                y[r][:, t] += z[e][:, fill[e]].astype(np.float64)
                fill[e] += 1
    return {"y": y.astype(z.dtype)}

from concourse.bass import DstId, RemoteDMATransfer
from concourse.mybir import AluOpType

SCRATCH = {
    "zs": ("sbuf", [128, 70], "float32"),
    "pq": ("sbuf", [128, 64], "float32"),
}
SEMAPHORES = ["loaded", "arrived", "placed", "sent", "summed", "stored"]


def find_runs(route):
    n = len(route)
    fill = [0] * n
    runs = []
    for r in range(n):
        live = {}
        for t, pair in enumerate(route[r]):
            now = {}
            for e in pair:
                if e in live:
                    now[e] = live[e]
            for e in pair:
                if e not in now:
                    taken = [x["h"] for x in now.values()]
                    run = {"e": e, "r": r, "t": t, "w": 0, "c": fill[e], "h": 1 if 0 in taken else 0}
                    now[e] = run
                    runs.append(run)
            for e in pair:
                now[e]["w"] += 1
                fill[e] += 1
            live = now
    return runs, fill


def plan_calls(runs, e):
    widths = {}
    for x in runs:
        if x["e"] == e and x["r"] != e:
            widths.setdefault(x["w"], []).append(x)
    calls = []
    for w in sorted(widths):
        todo = widths[w]
        ncalls = (len(todo) + 15) // 16
        for i in range(ncalls):
            part = todo[i::ncalls]
            eng = 16
            while eng * len(part) > 16:
                eng //= 2
            calls.append((eng, part))
    return calls


def rank_program(g, core, T, topo):
    me = T.rank_of(core)
    if me is None:
        return
    route = T.tables["ROUTE"]
    ntok = T.tables["T"]
    n = len(route)
    runs, fill = find_runs(route)
    S = T.sem

    g.sync.dma_start(T.zs[:, 0:fill[me]], T.z[:, 0:fill[me]]).then_inc(S.loaded, 16)
    g.wait_ge(S.loaded, 16)
    g.sync.wait_ge(S.loaded, 16)
    g.scalar.wait_ge(S.loaded, 16)

    def src_of(x):
        return T.zs[:, x["c"]:x["c"] + x["w"]]

    def dst_of(x):
        a = x["h"] * ntok + x["t"]
        return T.pq[:, a:a + x["w"]]

    sent = 0
    for eng, part in plan_calls(runs, me):
        transfers = []
        for i, x in enumerate(part):
            rid, pid, _se = topo.addr(T.cores[x["r"]])
            transfers.append(RemoteDMATransfer(
                dst_ids=[DstId(rid=rid, pnc=pid)],
                dma_engine_mask=((1 << eng) - 1) << (i * eng),
                remote_sem=S.arrived,
                src=src_of(x),
                dst=dst_of(x),
            ))
            sent += eng
        g.remote_dma_fused(transfers, local_sem=S.sent)

    own = [x for x in runs if x["e"] == me and x["r"] == me]
    for i, x in enumerate(own):
        q = g.sync if i % 2 == 0 else g.scalar
        q.dma_start(dst_of(x), src_of(x)).then_inc(S.placed, 16)

    expect = 0
    for e in range(n):
        if e != me:
            for eng, part in plan_calls(runs, e):
                expect += eng * sum(1 for x in part if x["r"] == me)
    g.wait_ge(S.placed, 16 * len(own))
    g.wait_ge(S.arrived, expect)
    g.dma_start(T.pq[:, 0:ntok], T.pq[:, ntok:2 * ntok], accum_op=AluOpType.add).then_inc(S.summed, 16)
    g.wait_ge(S.summed, 16)

    g.dma_start(T.y[:], T.pq[:, 0:ntok]).then_inc(S.stored, 16)
    g.wait_ge(S.stored, 16)
    g.wait_ge(S.sent, sent)
